import numpy as np
import ml_dtypes


def mxq(x, axis, fmt="e4m3"):
    dtype, down = {"e4m3": (ml_dtypes.float8_e4m3fn, 7), "e5m2": (ml_dtypes.float8_e5m2, 14)}[fmt]
    v = np.moveaxis(np.asarray(x, np.float32).astype(ml_dtypes.bfloat16).astype(np.float64), axis, -1)
    blocks = v.reshape(v.shape[:-1] + (-1, 32))
    amax = np.abs(blocks).max(-1, keepdims=True)
    byte = np.maximum(np.where(amax > 0, np.frexp(amax)[1] - 1 + 127, 0) - down, 1)
    scale = np.exp2(byte - 127.0)
    codes = (blocks / scale).astype(np.float32).astype(dtype).astype(np.float64)
    return np.moveaxis((codes * scale).reshape(v.shape), -1, axis)


WIDE = False


def mx_kscale(k):
    if not WIDE:
        return np.ones(k)
    levels = np.array([10, -10, 5, -5, 0])
    if k % 512:
        return np.exp2(np.random.permutation(np.resize(levels, k // 32))).repeat(32)
    a = np.empty((k // 512, 16))
    for p in range(k // 512):
        a[p, :8] = np.random.permutation(np.resize(levels, 8))
        for g in range(8):
            far = levels[np.abs(levels - a[p, g]) >= 10]
            a[p, g + 8] = far[np.random.randint(len(far))]
    return np.exp2(a.ravel()).repeat(32)


def f64(x):
    return np.asarray(x).astype(np.float64)


def striped8(idx):
    return np.asarray(idx).reshape(8, -1, 16).transpose(0, 2, 1).reshape(128, -1).astype(np.uint16)


def unstriped8(offs):
    return offs.reshape(8, 16, -1).transpose(0, 2, 1).reshape(8, -1).astype(np.int64)


def pick8(x, idx, run):
    r = np.arange(len(x))
    return x[r[:, None], idx[r % (8 * run) // run]]


E2M1 = np.array([0.0, 0.5, 1.0, 1.5, 2.0, 3.0, 4.0, 6.0, -0.0, -0.5, -1.0, -1.5, -2.0, -3.0, -4.0, -6.0])


def pack_weight(w, fmt):
    k, n = w.shape
    w = f64(np.asarray(w, np.float32).astype(ml_dtypes.bfloat16)).reshape(k // 32, 32, n)
    amax = np.abs(w).max(1)
    if fmt == "e4m3":
        byte = np.frexp(amax)[1] - 1 + 127 - 7
    else:
        mant, ex = np.frexp(amax / 6.0)
        byte = np.where(mant > 0.5, ex, ex - 1) + 127
    byte = np.clip(np.where(amax > 0, byte, 1), 1, 254)
    scaled = (w * np.exp2(127.0 - byte)[:, None, :]).reshape(k, n).astype(np.float32)
    by_word = np.ascontiguousarray(scaled.reshape(k // 512, 128, 4, n).transpose(0, 1, 3, 2))
    if fmt == "e4m3":
        words = by_word.astype(ml_dtypes.float8_e4m3fn).view(np.uint8)
    else:
        c = by_word.astype(ml_dtypes.float4_e2m1fn).view(np.uint8) & 0xF
        words = (c[..., 0::2] | (c[..., 1::2] << 4)).reshape(k // 512, 128, 2 * n)
    return np.ascontiguousarray(words), np.ascontiguousarray(byte.astype(np.uint8).reshape(k // 512, 16, n))


def unpack_weight(words, scales, fmt):
    g, _, n = scales.shape
    words = np.ascontiguousarray(words).reshape(g, 128, n, -1)
    if fmt == "e4m3":
        vals = words.view(ml_dtypes.float8_e4m3fn).astype(np.float64)
    else:
        nib = np.empty((g, 128, n, 4), np.uint8)
        nib[..., 0::2] = words & 0xF
        nib[..., 1::2] = words >> 4
        vals = E2M1[nib]
    vals = vals * np.repeat(np.exp2(scales.astype(np.float64) - 127.0), 8, axis=1)[..., None]
    return vals.transpose(0, 1, 3, 2).reshape(g * 512, n)


D, T, U, I, Q = 512, 1024, 1024, 512, 128


def setup_inputs():
    n = np.random.standard_normal
    idx = np.stack([np.random.permutation(T)[:I] for _ in range(8)])
    idx2 = np.stack([np.random.permutation(U)[:I] for _ in range(8)])
    idx3 = np.stack([np.random.permutation(U)[:I] for _ in range(8)])
    idx4 = np.stack([np.random.permutation(T)[:I] for _ in range(8)])
    idx5 = np.stack([np.random.permutation(U)[:I] for _ in range(8)])
    idx6 = np.stack([np.random.permutation(T)[:I] for _ in range(8)])
    fd = mx_kscale(D)
    keysp = pack_weight(n((D, T)) / fd[:, None], "e4m3")
    notesp = pack_weight(n((D, U)) / fd[:, None], "e2m1")
    return {
        "query": (n((D, Q)) * 1.0 / np.sqrt(D) * fd[:, None]).astype(np.float32),
        "keys_words": keysp[0],
        "keys_scales": keysp[1],
        "notes_words": notesp[0],
        "notes_scales": notesp[1],
        "offs": striped8(idx),
        "offs2": striped8(idx2),
        "offs3": striped8(idx3),
        "offs4": striped8(idx4),
        "offs5": striped8(idx5),
        "offs6": striped8(idx6),
    }


def reference(query, keys_words, keys_scales, notes_words, notes_scales, offs, offs2, offs3, offs4, offs5, offs6):
    idx = unstriped8(offs)
    idx2 = unstriped8(offs2)
    idx3 = unstriped8(offs3)
    idx4 = unstriped8(offs4)
    idx5 = unstriped8(offs5)
    idx6 = unstriped8(offs6)
    keysu = unpack_weight(keys_words, keys_scales, "e4m3")
    notesu = unpack_weight(notes_words, notes_scales, "e2m1")
    queryq = mxq(f64(query), 0, "e4m3")
    a = queryq.T @ keysu
    b = queryq.T @ notesu
    f1 = np.zeros((Q, U))
    f1[np.arange(Q)[:, None], idx2[np.arange(Q) % 128 // 16]] = pick8(a, idx, 16)
    bb = b + f1
    f2 = np.zeros((Q, T))
    f2[np.arange(Q)[:, None], idx4[np.arange(Q) % 128 // 16]] = pick8(bb, idx3, 16)
    f3 = np.zeros((Q, T))
    f3[np.arange(Q)[:, None], idx6[np.arange(Q) % 128 // 16]] = pick8(bb, idx5, 16)
    m1 = np.maximum(f2, f3)
    aa = a - m1
    y = pick8(aa, idx, 16)
    return y

@@ -1,0 +1,158 @@
+from contextlib import ExitStack
+
+import concourse.mybir as mybir
+
+D, T, U, I, Q = 512, 1024, 1024, 512, 128
+FLOPS = 2 * D * Q * (T + U)
+
+F32 = mybir.dt.float32
+BF16 = mybir.dt.bfloat16
+I32 = mybir.dt.int32
+U32 = mybir.dt.uint32
+U16 = mybir.dt.uint16
+U8 = mybir.dt.uint8
+FP8X4 = mybir.dt.float8_e4m3fn_x4
+FP4X4 = mybir.dt.float4_e2m1fn_x4
+ALU = mybir.AluOpType
+COPY = mybir.ActivationFunctionType.Copy
+
+P = 128
+PACK = 4
+LANES = 16
+HALF = I // 2
+KEY_N = 256
+NOTE_N = 512
+
+
+def tile_attend_tworelays_two_kernel(
+    tc, query, keys_words, keys_scales, notes_words, notes_scales, offs, offs2, offs3, offs4, offs5, offs6, out
+):
+    nc = tc.nc
+    with ExitStack() as ctx:
+        lists = ctx.enter_context(tc.tile_pool(name="lists", bufs=1))
+        sb = ctx.enter_context(tc.tile_pool(name="sb", bufs=1))
+        psum = ctx.enter_context(tc.psum_pool(name="psum", bufs=1))
+
+        def load_list(src, name):
+            t = lists.tile([P, I // LANES], U16, name=name)
+            nc.sync.dma_start(t[:], src)
+            return t
+
+        def gather_halves(dst, window, lst):
+            h = HALF // LANES
+            nc.vector.tensor_copy(dst[:, :HALF], window[:].indirect(lst[:, :h]))
+            nc.scalar.activation(dst[:, HALF:], window[:].indirect(lst[:, h:]), COPY)
+
+        key_scales = sb.tile([P, KEY_N], U8, name="key_scales", align_bytes=64)
+        nc.vector.memset(key_scales[:].bitcast(U32), 0)
+
+        q_raw = sb.tile([P, PACK, Q], F32, name="q_raw")
+        nc.sync.dma_start(q_raw[:], query.rearrange("(p j) q -> p j q", j=PACK))
+
+        ks_rows = keys_scales[0].bitcast(I32)
+        for quad in range(4):
+            nc.scalar.dma_start(
+                key_scales[32 * quad : 32 * quad + 16, :].bitcast(I32),
+                ks_rows[4 * quad : 4 * quad + 4, :].rearrange("r (c n) -> c r n", c=T // KEY_N),
+            )
+
+        kw_rows = keys_words[0].rearrange("p n t -> p (n t)").bitcast(I32)
+        key_words = []
+        for h in range(2):
+            kw = sb.tile([P, T // 2], U32, name="key_words%d" % h, align_bytes=64)
+            nc.sync.dma_start(kw[:].bitcast(I32), kw_rows[:, h * (T // 2) : (h + 1) * (T // 2)])
+            key_words.append(kw)
+
+        idx = load_list(offs, "idx")
+        idx2 = load_list(offs2, "idx2")
+
+        f1 = sb.tile([P, U], F32, name="f1")
+        nc.vector.memset(f1[:], 0.0)
+        note_scales = sb.tile([P, U], U8, name="note_scales", align_bytes=64)
+        nc.vector.memset(note_scales[:].bitcast(U32), 0)
+        f2 = sb.tile([P, T], F32, name="f2")
+        nc.vector.memset(f2[:], 0.0)
+        f3 = sb.tile([P, T], F32, name="f3")
+        nc.vector.memset(f3[:], 0.0)
+
+        note_words = sb.tile([P, 2 * U], U8, name="note_words", align_bytes=64)
+        nc.sync.dma_start(note_words[:].bitcast(I32), notes_words[0].bitcast(I32))
+        ns_rows = notes_scales[0].bitcast(I32)
+        for quad in range(4):
+            nc.sync.dma_start(
+                note_scales[32 * quad : 32 * quad + 4, :].bitcast(I32), ns_rows[4 * quad : 4 * quad + 4, :]
+            )
+        idx3 = load_list(offs3, "idx3")
+        idx5 = load_list(offs5, "idx5")
+        idx4 = load_list(offs4, "idx4")
+        idx6 = load_list(offs6, "idx6")
+
+        q_bf = sb.tile([P, Q, PACK], BF16, name="q_bf", align_bytes=64)
+        nc.vector.tensor_copy(q_bf[:], q_raw[:].rearrange("p j q -> p q j"))
+        q_words = sb.tile([P, Q], U32, name="q_words", align_bytes=64)
+        q_scales = sb.tile([P, Q], U8, name="q_scales", align_bytes=64)
+        nc.vector.quantize_mx(
+            out=q_words[:].bitcast(FP8X4), scales=q_scales[:], in_=q_bf[:].rearrange("p q j -> p (q j)")
+        )
+
+        a = sb.tile([P, T], F32, name="a")
+        for c in range(T // KEY_N):
+            bank = psum.tile([P, KEY_N], F32, name="a_bank%d" % c)
+            col = (c % 2) * KEY_N
+            nc.tensor.matmul_mx(
+                out=bank[:],
+                lhsT=q_words[:].bitcast(FP8X4),
+                lhsT_scale=q_scales[:],
+                rhs=key_words[c // 2][:, col : col + KEY_N].bitcast(FP8X4),
+                rhs_scale=key_scales[4 * c : P, :],
+                start=True,
+                stop=True,
+            )
+            cols = slice(c * KEY_N, (c + 1) * KEY_N)
+            if c % 2 == 0:
+                nc.scalar.activation(a[:, cols], bank[:], COPY)
+            else:
+                nc.vector.tensor_copy(a[:, cols], bank[:])
+
+        b_banks = []
+        for c in range(U // NOTE_N):
+            bank = psum.tile([P, NOTE_N], F32, name="b_bank%d" % c)
+            nc.tensor.matmul_mx(
+                out=bank[:],
+                lhsT=q_words[:].bitcast(FP8X4),
+                lhsT_scale=q_scales[:],
+                rhs=note_words[:, 2 * NOTE_N * c : 2 * NOTE_N * (c + 1)].bitcast(FP4X4),
+                rhs_scale=note_scales[:, NOTE_N * c : NOTE_N * (c + 1)],
+                start=True,
+                stop=True,
+            )
+            b_banks.append(bank)
+
+        a_picked = sb.tile([P, I], F32, name="a_picked")
+        gather_halves(a_picked, a, idx)
+        nc.vector.tensor_copy(f1[:].indirect(idx2[:]), a_picked[:])
+
+        bb = sb.tile([P, U], F32, name="bb")
+        for c in range(U // NOTE_N):
+            cols = slice(c * NOTE_N, (c + 1) * NOTE_N)
+            nc.vector.tensor_tensor(bb[:, cols], b_banks[c][:], f1[:, cols], ALU.add)
+
+        relay2 = sb.tile([P, I], F32, name="relay2")
+        gather_halves(relay2, bb, idx3)
+        relay3 = sb.tile([P, I], F32, name="relay3")
+        nc.scalar.activation(relay3[:], bb[:].indirect(idx5[:]), COPY)
+        nc.vector.tensor_copy(f2[:].indirect(idx4[:]), relay2[:])
+        nc.vector.tensor_copy(f3[:].indirect(idx6[:]), relay3[:])
+
+        m1 = sb.tile([P, T], F32, name="m1")
+        aa = sb.tile([P, T], F32, name="aa")
+        halves = [slice(0, T // 2), slice(T // 2, T)]
+        for cols in halves:
+            nc.vector.tensor_tensor(m1[:, cols], f2[:, cols], f3[:, cols], ALU.max)
+        for cols in halves:
+            nc.vector.tensor_tensor(aa[:, cols], a[:, cols], m1[:, cols], ALU.subtract)
+
+        y = sb.tile([P, I], F32, name="y")
+        gather_halves(y, aa, idx)
+        nc.sync.dma_start(out[:, :HALF], y[:, :HALF])
+        nc.scalar.dma_start(out[:, HALF:], y[:, HALF:])

@@ -22,6 +22,7 @@ LANES = 16
 HALF = I // 2
 KEY_N = 256
 NOTE_N = 512
+FIRST = 128
 
 
 def tile_attend_tworelays_two_kernel(
@@ -44,14 +45,13 @@ def tile_attend_tworelays_two_kernel(
             nc.scalar.activation(dst[:, HALF:], window[:].indirect(lst[:, h:]), COPY)
 
         key_scales = sb.tile([P, KEY_N], U8, name="key_scales", align_bytes=64)
-        nc.vector.memset(key_scales[:].bitcast(U32), 0)
 
         q_raw = sb.tile([P, PACK, Q], F32, name="q_raw")
         nc.sync.dma_start(q_raw[:], query.rearrange("(p j) q -> p j q", j=PACK))
 
         ks_rows = keys_scales[0].bitcast(I32)
         for quad in range(4):
-            nc.scalar.dma_start(
+            (nc.sync if quad < 2 else nc.scalar).dma_start(
                 key_scales[32 * quad : 32 * quad + 16, :].bitcast(I32),
                 ks_rows[4 * quad : 4 * quad + 4, :].rearrange("r (c n) -> c r n", c=T // KEY_N),
             )
@@ -69,11 +69,10 @@ def tile_attend_tworelays_two_kernel(
         f1 = sb.tile([P, U], F32, name="f1")
         nc.vector.memset(f1[:], 0.0)
         note_scales = sb.tile([P, U], U8, name="note_scales", align_bytes=64)
-        nc.vector.memset(note_scales[:].bitcast(U32), 0)
         f2 = sb.tile([P, T], F32, name="f2")
         nc.vector.memset(f2[:], 0.0)
-        f3 = sb.tile([P, T], F32, name="f3")
-        nc.vector.memset(f3[:], 0.0)
+        ones = sb.tile([P, FIRST], F32, name="ones")
+        nc.vector.memset(ones[:], 1.0)
 
         note_words = sb.tile([P, 2 * U], U8, name="note_words", align_bytes=64)
         nc.sync.dma_start(note_words[:].bitcast(I32), notes_words[0].bitcast(I32))
@@ -87,29 +86,39 @@ def tile_attend_tworelays_two_kernel(
         idx4 = load_list(offs4, "idx4")
         idx6 = load_list(offs6, "idx6")
 
-        q_bf = sb.tile([P, Q, PACK], BF16, name="q_bf", align_bytes=64)
-        nc.vector.tensor_copy(q_bf[:], q_raw[:].rearrange("p j q -> p q j"))
+        q_bf = sb.tile([P, Q, PACK], BF16, name="q_bf", tag="q_bf_then_f3", align_bytes=64)
         q_words = sb.tile([P, Q], U32, name="q_words", align_bytes=64)
         q_scales = sb.tile([P, Q], U8, name="q_scales", align_bytes=64)
-        nc.vector.quantize_mx(
-            out=q_words[:].bitcast(FP8X4), scales=q_scales[:], in_=q_bf[:].rearrange("p q j -> p (q j)")
-        )
+        q_halves = [slice(0, Q // 2), slice(Q // 2, Q)]
+        for rows in q_halves:
+            nc.vector.tensor_copy(q_bf[:, rows, :], q_raw[:, :, rows].rearrange("p j q -> p q j"))
+        for rows in q_halves:
+            nc.vector.quantize_mx(
+                out=q_words[:, rows].bitcast(FP8X4),
+                scales=q_scales[:, rows],
+                in_=q_bf[:, rows, :].rearrange("p q j -> p (q j)"),
+            )
+        f3 = sb.tile([P, T], F32, name="f3", tag="q_bf_then_f3", align_bytes=64)
+        nc.vector.memset(f3[:], 0.0)
 
         a = sb.tile([P, T], F32, name="a")
-        for c in range(T // KEY_N):
-            bank = psum.tile([P, KEY_N], F32, name="a_bank%d" % c)
-            col = (c % 2) * KEY_N
+        pieces = [(0, 256, "s"), (256, 256, "s"), (512, 256, "v"), (768, 128, "s"), (896, 128, "v")]
+        for start, width, eng in pieces:
+            bank = psum.tile([P, width], F32, name="a_bank%d" % start)
+            c = start // KEY_N
+            wcol = start % (T // 2)
+            scol = start % KEY_N
             nc.tensor.matmul_mx(
                 out=bank[:],
                 lhsT=q_words[:].bitcast(FP8X4),
                 lhsT_scale=q_scales[:],
-                rhs=key_words[c // 2][:, col : col + KEY_N].bitcast(FP8X4),
-                rhs_scale=key_scales[4 * c : P, :],
+                rhs=key_words[c // 2][:, wcol : wcol + width].bitcast(FP8X4),
+                rhs_scale=key_scales[4 * c : P, scol : scol + width],
                 start=True,
                 stop=True,
             )
-            cols = slice(c * KEY_N, (c + 1) * KEY_N)
-            if c % 2 == 0:
+            cols = slice(start, start + width)
+            if eng == "s":
                 nc.scalar.activation(a[:, cols], bank[:], COPY)
             else:
                 nc.vector.tensor_copy(a[:, cols], bank[:])
@@ -137,12 +146,21 @@ def tile_attend_tworelays_two_kernel(
             cols = slice(c * NOTE_N, (c + 1) * NOTE_N)
             nc.vector.tensor_tensor(bb[:, cols], b_banks[c][:], f1[:, cols], ALU.add)
 
-        relay2 = sb.tile([P, I], F32, name="relay2")
-        gather_halves(relay2, bb, idx3)
-        relay3 = sb.tile([P, I], F32, name="relay3")
-        nc.scalar.activation(relay3[:], bb[:].indirect(idx5[:]), COPY)
-        nc.vector.tensor_copy(f2[:].indirect(idx4[:]), relay2[:])
-        nc.vector.tensor_copy(f3[:].indirect(idx6[:]), relay3[:])
+        def lcols(lo, hi):
+            return slice(lo // LANES, hi // LANES)
+
+        r2a = sb.tile([P, FIRST], F32, name="r2a")
+        r2b = sb.tile([P, I - FIRST], F32, name="r2b")
+        r3a = sb.tile([P, HALF], F32, name="r3a")
+        r3b = sb.tile([P, HALF], F32, name="r3b")
+        nc.vector.tensor_tensor(r2a[:], bb[:].indirect(idx3[:, lcols(0, FIRST)]), ones[:], ALU.mult)
+        nc.scalar.activation(r3a[:], bb[:].indirect(idx5[:, lcols(0, HALF)]), COPY)
+        nc.scalar.activation(r2b[:], bb[:].indirect(idx3[:, lcols(FIRST, I)]), COPY)
+        nc.scalar.activation(r3b[:], bb[:].indirect(idx5[:, lcols(HALF, I)]), COPY)
+        nc.vector.tensor_copy(f2[:].indirect(idx4[:, lcols(0, FIRST)]), r2a[:])
+        nc.vector.tensor_copy(f3[:].indirect(idx6[:, lcols(0, HALF)]), r3a[:])
+        nc.vector.tensor_copy(f2[:].indirect(idx4[:, lcols(FIRST, I)]), r2b[:])
+        nc.vector.tensor_copy(f3[:].indirect(idx6[:, lcols(HALF, I)]), r3b[:])
 
         m1 = sb.tile([P, T], F32, name="m1")
         aa = sb.tile([P, T], F32, name="aa")

@@ -23,6 +23,7 @@ HALF = I // 2
 KEY_N = 256
 NOTE_N = 512
 FIRST = 128
+SPLIT = 704
 
 
 def tile_attend_tworelays_two_kernel(
@@ -67,7 +68,7 @@ def tile_attend_tworelays_two_kernel(
         idx2 = load_list(offs2, "idx2")
 
         f1 = sb.tile([P, U], F32, name="f1")
-        nc.vector.memset(f1[:], 0.0)
+        nc.gpsimd.memset(f1[:], 0.0)
         note_scales = sb.tile([P, U], U8, name="note_scales", align_bytes=64)
         f2 = sb.tile([P, T], F32, name="f2")
         nc.vector.memset(f2[:], 0.0)
@@ -99,10 +100,11 @@ def tile_attend_tworelays_two_kernel(
                 in_=q_bf[:, rows, :].rearrange("p q j -> p (q j)"),
             )
         f3 = sb.tile([P, T], F32, name="f3", tag="q_bf_then_f3", align_bytes=64)
-        nc.vector.memset(f3[:], 0.0)
+        nc.gpsimd.memset(f3[:], 0.0)
 
         a = sb.tile([P, T], F32, name="a")
-        pieces = [(0, 256, "s"), (256, 256, "s"), (512, 256, "v"), (768, 128, "s"), (896, 128, "v")]
+        pieces = [(0, 256, "v"), (256, 256, "s"), (512, 256, "v"), (768, 128, "s"), (896, 128, "v")]
+        a_banks = []
         for start, width, eng in pieces:
             bank = psum.tile([P, width], F32, name="a_bank%d" % start)
             c = start // KEY_N
@@ -117,6 +119,7 @@ def tile_attend_tworelays_two_kernel(
                 start=True,
                 stop=True,
             )
+            a_banks.append(bank)
             cols = slice(start, start + width)
             if eng == "s":
                 nc.scalar.activation(a[:, cols], bank[:], COPY)
@@ -141,10 +144,12 @@ def tile_attend_tworelays_two_kernel(
         gather_halves(a_picked, a, idx)
         nc.vector.tensor_copy(f1[:].indirect(idx2[:]), a_picked[:])
 
+        b_tail = sb.tile([P, U - SPLIT], F32, name="b_tail")
+        nc.scalar.activation(b_tail[:], b_banks[1][:, SPLIT - NOTE_N :], COPY)
         bb = sb.tile([P, U], F32, name="bb")
-        for c in range(U // NOTE_N):
-            cols = slice(c * NOTE_N, (c + 1) * NOTE_N)
-            nc.vector.tensor_tensor(bb[:, cols], b_banks[c][:], f1[:, cols], ALU.add)
+        nc.gpsimd.tensor_tensor(bb[:, SPLIT:], b_tail[:], f1[:, SPLIT:], ALU.add)
+        nc.vector.tensor_tensor(bb[:, :NOTE_N], b_banks[0][:], f1[:, :NOTE_N], ALU.add)
+        nc.vector.tensor_tensor(bb[:, NOTE_N:SPLIT], b_banks[1][:, : SPLIT - NOTE_N], f1[:, NOTE_N:SPLIT], ALU.add)
 
         def lcols(lo, hi):
             return slice(lo // LANES, hi // LANES)
@@ -164,11 +169,12 @@ def tile_attend_tworelays_two_kernel(
 
         m1 = sb.tile([P, T], F32, name="m1")
         aa = sb.tile([P, T], F32, name="aa")
-        halves = [slice(0, T // 2), slice(T // 2, T)]
-        for cols in halves:
+        for cols in (slice(0, KEY_N), slice(SPLIT, T), slice(KEY_N, SPLIT)):
             nc.vector.tensor_tensor(m1[:, cols], f2[:, cols], f3[:, cols], ALU.max)
-        for cols in halves:
-            nc.vector.tensor_tensor(aa[:, cols], a[:, cols], m1[:, cols], ALU.subtract)
+        nc.gpsimd.tensor_tensor(aa[:, SPLIT:], a[:, SPLIT:], m1[:, SPLIT:], ALU.subtract)
+        for c in range(3):
+            lo, hi = c * KEY_N, min((c + 1) * KEY_N, SPLIT)
+            nc.vector.tensor_tensor(aa[:, lo:hi], a_banks[c][:, : hi - lo], m1[:, lo:hi], ALU.subtract)
 
         y = sb.tile([P, I], F32, name="y")
         gather_halves(y, aa, idx)

@@ -18,12 +18,20 @@ COPY = mybir.ActivationFunctionType.Copy
 
 P = 128
 PACK = 4
-LANES = 16
+QUADS = 4
+QUAD_ROWS = 4
+LIST_ROWS = 16
 HALF = I // 2
-KEY_N = 256
-NOTE_N = 512
-FIRST = 128
+SMALL = 128
+KEY_CHUNK = 256
+NOTE_CHUNK = 512
 SPLIT = 704
+KEY_LOADS = ((0, 256), (256, 256), (512, 512))
+KEY_MATMULS = ((0, 256), (256, 256), (512, 256), (768, 128), (896, 128))
+
+
+def slots(lst, lo, hi):
+    return lst[:, lo // LIST_ROWS : hi // LIST_ROWS]
 
 
 def tile_attend_tworelays_two_kernel(
@@ -36,51 +44,57 @@ def tile_attend_tworelays_two_kernel(
         psum = ctx.enter_context(tc.psum_pool(name="psum", bufs=1))
 
         def load_list(src, name):
-            t = lists.tile([P, I // LANES], U16, name=name)
-            nc.sync.dma_start(t[:], src)
-            return t
+            lst = lists.tile([P, I // LIST_ROWS], U16, name=name)
+            nc.sync.dma_start(lst[:], src)
+            return lst
 
-        def gather_halves(dst, window, lst):
-            h = HALF // LANES
-            nc.vector.tensor_copy(dst[:, :HALF], window[:].indirect(lst[:, :h]))
-            nc.scalar.activation(dst[:, HALF:], window[:].indirect(lst[:, h:]), COPY)
+        def gather_small(dst, window, offsets):
+            nc.vector.tensor_tensor(dst, window[:].indirect(offsets), ones[:], ALU.mult)
 
-        key_scales = sb.tile([P, KEY_N], U8, name="key_scales", align_bytes=64)
+        def gather_scalar(dst, window, offsets):
+            nc.scalar.activation(dst, window[:].indirect(offsets), COPY)
+
+        def scatter(window, offsets, src):
+            nc.vector.tensor_copy(window[:].indirect(offsets), src)
 
         q_raw = sb.tile([P, PACK, Q], F32, name="q_raw")
         nc.sync.dma_start(q_raw[:], query.rearrange("(p j) q -> p j q", j=PACK))
 
+        key_scales = sb.tile([P, KEY_CHUNK], U8, name="key_scales", align_bytes=64)
         ks_rows = keys_scales[0].bitcast(I32)
-        for quad in range(4):
-            (nc.sync if quad < 2 else nc.scalar).dma_start(
-                key_scales[32 * quad : 32 * quad + 16, :].bitcast(I32),
-                ks_rows[4 * quad : 4 * quad + 4, :].rearrange("r (c n) -> c r n", c=T // KEY_N),
+        planes = T // KEY_CHUNK
+        for quad in range(QUADS):
+            queue = nc.sync if quad < QUADS // 2 else nc.scalar
+            queue.dma_start(
+                key_scales[32 * quad : 32 * quad + planes * QUAD_ROWS, :].bitcast(I32),
+                ks_rows[QUAD_ROWS * quad : QUAD_ROWS * (quad + 1), :].rearrange("r (c n) -> c r n", c=planes),
             )
 
         kw_rows = keys_words[0].rearrange("p n t -> p (n t)").bitcast(I32)
         key_words = []
-        for h in range(2):
-            kw = sb.tile([P, T // 2], U32, name="key_words%d" % h, align_bytes=64)
-            nc.sync.dma_start(kw[:].bitcast(I32), kw_rows[:, h * (T // 2) : (h + 1) * (T // 2)])
-            key_words.append(kw)
+        for first, width in KEY_LOADS:
+            words = sb.tile([P, width], U32, name="key_words%d" % first, align_bytes=64)
+            nc.sync.dma_start(words[:].bitcast(I32), kw_rows[:, first : first + width])
+            key_words.append(words)
 
         idx = load_list(offs, "idx")
         idx2 = load_list(offs2, "idx2")
 
         f1 = sb.tile([P, U], F32, name="f1")
         nc.gpsimd.memset(f1[:], 0.0)
-        note_scales = sb.tile([P, U], U8, name="note_scales", align_bytes=64)
         f2 = sb.tile([P, T], F32, name="f2")
         nc.vector.memset(f2[:], 0.0)
-        ones = sb.tile([P, FIRST], F32, name="ones")
+        ones = sb.tile([P, SMALL], F32, name="ones")
         nc.vector.memset(ones[:], 1.0)
 
         note_words = sb.tile([P, 2 * U], U8, name="note_words", align_bytes=64)
         nc.sync.dma_start(note_words[:].bitcast(I32), notes_words[0].bitcast(I32))
+        note_scales = sb.tile([P, U], U8, name="note_scales", align_bytes=64)
         ns_rows = notes_scales[0].bitcast(I32)
-        for quad in range(4):
+        for quad in range(QUADS):
             nc.sync.dma_start(
-                note_scales[32 * quad : 32 * quad + 4, :].bitcast(I32), ns_rows[4 * quad : 4 * quad + 4, :]
+                note_scales[32 * quad : 32 * quad + QUAD_ROWS, :].bitcast(I32),
+                ns_rows[QUAD_ROWS * quad : QUAD_ROWS * (quad + 1), :],
             )
         idx3 = load_list(offs3, "idx3")
         idx5 = load_list(offs5, "idx5")
@@ -90,9 +104,12 @@ def tile_attend_tworelays_two_kernel(
         q_bf = sb.tile([P, Q, PACK], BF16, name="q_bf", tag="q_bf_then_f3", align_bytes=64)
         q_words = sb.tile([P, Q], U32, name="q_words", align_bytes=64)
         q_scales = sb.tile([P, Q], U8, name="q_scales", align_bytes=64)
-        q_halves = [slice(0, Q // 2), slice(Q // 2, Q)]
+        q_halves = (slice(0, Q // 2), slice(Q // 2, Q))
         for rows in q_halves:
-            nc.vector.tensor_copy(q_bf[:, rows, :], q_raw[:, :, rows].rearrange("p j q -> p q j"))
+            nc.vector.tensor_copy(
+                q_bf[:, rows, :].rearrange("p (c i) j -> p c j i", i=4),
+                q_raw[:, :, rows].rearrange("p j (c i) -> p c j i", i=4),
+            )
         for rows in q_halves:
             nc.vector.quantize_mx(
                 out=q_words[:, rows].bitcast(FP8X4),
@@ -102,81 +119,85 @@ def tile_attend_tworelays_two_kernel(
         f3 = sb.tile([P, T], F32, name="f3", tag="q_bf_then_f3", align_bytes=64)
         nc.gpsimd.memset(f3[:], 0.0)
 
-        a = sb.tile([P, T], F32, name="a")
-        pieces = [(0, 256, "v"), (256, 256, "s"), (512, 256, "v"), (768, 128, "s"), (896, 128, "v")]
-        a_banks = []
-        for start, width, eng in pieces:
-            bank = psum.tile([P, width], F32, name="a_bank%d" % start)
-            c = start // KEY_N
-            wcol = start % (T // 2)
-            scol = start % KEY_N
+        def scores(bank, words, scales):
             nc.tensor.matmul_mx(
                 out=bank[:],
                 lhsT=q_words[:].bitcast(FP8X4),
                 lhsT_scale=q_scales[:],
-                rhs=key_words[c // 2][:, wcol : wcol + width].bitcast(FP8X4),
-                rhs_scale=key_scales[4 * c : P, scol : scol + width],
+                rhs=words,
+                rhs_scale=scales,
                 start=True,
                 stop=True,
             )
+
+        a = sb.tile([P, T], F32, name="a")
+        a_banks = []
+        for n, (first, width) in enumerate(KEY_MATMULS):
+            load = max(k for k, (lo, w) in enumerate(KEY_LOADS) if lo <= first)
+            in_load = first - KEY_LOADS[load][0]
+            plane, in_plane = divmod(first, KEY_CHUNK)
+            bank = psum.tile([P, width], F32, name="a_bank%d" % first)
+            scores(
+                bank,
+                key_words[load][:, in_load : in_load + width].bitcast(FP8X4),
+                key_scales[QUAD_ROWS * plane : P, in_plane : in_plane + width],
+            )
             a_banks.append(bank)
-            cols = slice(start, start + width)
-            if eng == "s":
-                nc.scalar.activation(a[:, cols], bank[:], COPY)
+            if n % 2 == 0:
+                nc.vector.tensor_copy(a[:, first : first + width], bank[:])
             else:
-                nc.vector.tensor_copy(a[:, cols], bank[:])
+                nc.scalar.activation(a[:, first : first + width], bank[:], COPY)
 
         b_banks = []
-        for c in range(U // NOTE_N):
-            bank = psum.tile([P, NOTE_N], F32, name="b_bank%d" % c)
-            nc.tensor.matmul_mx(
-                out=bank[:],
-                lhsT=q_words[:].bitcast(FP8X4),
-                lhsT_scale=q_scales[:],
-                rhs=note_words[:, 2 * NOTE_N * c : 2 * NOTE_N * (c + 1)].bitcast(FP4X4),
-                rhs_scale=note_scales[:, NOTE_N * c : NOTE_N * (c + 1)],
-                start=True,
-                stop=True,
+        for first in range(0, U, NOTE_CHUNK):
+            bank = psum.tile([P, NOTE_CHUNK], F32, name="b_bank%d" % first)
+            scores(
+                bank,
+                note_words[:, 2 * first : 2 * (first + NOTE_CHUNK)].bitcast(FP4X4),
+                note_scales[:, first : first + NOTE_CHUNK],
             )
             b_banks.append(bank)
 
         a_picked = sb.tile([P, I], F32, name="a_picked")
-        gather_halves(a_picked, a, idx)
-        nc.vector.tensor_copy(f1[:].indirect(idx2[:]), a_picked[:])
+        nc.vector.tensor_copy(a_picked[:, :HALF], a[:].indirect(slots(idx, 0, HALF)))
+        gather_scalar(a_picked[:, HALF:], a, slots(idx, HALF, I))
+        scatter(f1, idx2[:], a_picked[:])
 
         b_tail = sb.tile([P, U - SPLIT], F32, name="b_tail")
-        nc.scalar.activation(b_tail[:], b_banks[1][:, SPLIT - NOTE_N :], COPY)
+        nc.scalar.activation(b_tail[:], b_banks[1][:, SPLIT - NOTE_CHUNK :], COPY)
         bb = sb.tile([P, U], F32, name="bb")
         nc.gpsimd.tensor_tensor(bb[:, SPLIT:], b_tail[:], f1[:, SPLIT:], ALU.add)
-        nc.vector.tensor_tensor(bb[:, :NOTE_N], b_banks[0][:], f1[:, :NOTE_N], ALU.add)
-        nc.vector.tensor_tensor(bb[:, NOTE_N:SPLIT], b_banks[1][:, : SPLIT - NOTE_N], f1[:, NOTE_N:SPLIT], ALU.add)
+        nc.vector.tensor_tensor(bb[:, :NOTE_CHUNK], b_banks[0][:], f1[:, :NOTE_CHUNK], ALU.add)
+        nc.vector.tensor_tensor(
+            bb[:, NOTE_CHUNK:SPLIT], b_banks[1][:, : SPLIT - NOTE_CHUNK], f1[:, NOTE_CHUNK:SPLIT], ALU.add
+        )
 
-        def lcols(lo, hi):
-            return slice(lo // LANES, hi // LANES)
-
-        r2a = sb.tile([P, FIRST], F32, name="r2a")
-        r2b = sb.tile([P, I - FIRST], F32, name="r2b")
-        r3a = sb.tile([P, HALF], F32, name="r3a")
-        r3b = sb.tile([P, HALF], F32, name="r3b")
-        nc.vector.tensor_tensor(r2a[:], bb[:].indirect(idx3[:, lcols(0, FIRST)]), ones[:], ALU.mult)
-        nc.scalar.activation(r3a[:], bb[:].indirect(idx5[:, lcols(0, HALF)]), COPY)
-        nc.scalar.activation(r2b[:], bb[:].indirect(idx3[:, lcols(FIRST, I)]), COPY)
-        nc.scalar.activation(r3b[:], bb[:].indirect(idx5[:, lcols(HALF, I)]), COPY)
-        nc.vector.tensor_copy(f2[:].indirect(idx4[:, lcols(0, FIRST)]), r2a[:])
-        nc.vector.tensor_copy(f3[:].indirect(idx6[:, lcols(0, HALF)]), r3a[:])
-        nc.vector.tensor_copy(f2[:].indirect(idx4[:, lcols(FIRST, I)]), r2b[:])
-        nc.vector.tensor_copy(f3[:].indirect(idx6[:, lcols(HALF, I)]), r3b[:])
+        to_f2_a = sb.tile([P, SMALL], F32, name="to_f2_a")
+        to_f2_b = sb.tile([P, I - SMALL], F32, name="to_f2_b")
+        to_f3_a = sb.tile([P, HALF], F32, name="to_f3_a")
+        to_f3_b = sb.tile([P, HALF], F32, name="to_f3_b")
+        gather_small(to_f2_a[:], bb, slots(idx3, 0, SMALL))
+        gather_scalar(to_f3_a[:], bb, slots(idx5, 0, HALF))
+        gather_scalar(to_f2_b[:], bb, slots(idx3, SMALL, I))
+        gather_scalar(to_f3_b[:], bb, slots(idx5, HALF, I))
+        scatter(f2, slots(idx4, 0, SMALL), to_f2_a[:])
+        scatter(f3, slots(idx6, 0, HALF), to_f3_a[:])
+        scatter(f2, slots(idx4, SMALL, I), to_f2_b[:])
+        scatter(f3, slots(idx6, HALF, I), to_f3_b[:])
 
         m1 = sb.tile([P, T], F32, name="m1")
         aa = sb.tile([P, T], F32, name="aa")
-        for cols in (slice(0, KEY_N), slice(SPLIT, T), slice(KEY_N, SPLIT)):
+        for cols in (slice(0, KEY_CHUNK), slice(SPLIT, T), slice(KEY_CHUNK, SPLIT)):
             nc.vector.tensor_tensor(m1[:, cols], f2[:, cols], f3[:, cols], ALU.max)
         nc.gpsimd.tensor_tensor(aa[:, SPLIT:], a[:, SPLIT:], m1[:, SPLIT:], ALU.subtract)
-        for c in range(3):
-            lo, hi = c * KEY_N, min((c + 1) * KEY_N, SPLIT)
-            nc.vector.tensor_tensor(aa[:, lo:hi], a_banks[c][:, : hi - lo], m1[:, lo:hi], ALU.subtract)
+        for bank, (first, width) in zip(a_banks, KEY_MATMULS):
+            last = min(first + width, SPLIT)
+            if first < last:
+                nc.vector.tensor_tensor(aa[:, first:last], bank[:, : last - first], m1[:, first:last], ALU.subtract)
 
         y = sb.tile([P, I], F32, name="y")
-        gather_halves(y, aa, idx)
-        nc.sync.dma_start(out[:, :HALF], y[:, :HALF])
+        gather_scalar(y[:, HALF:], aa, slots(idx, HALF, I))
+        for first in range(0, HALF, SMALL):
+            gather_small(y[:, first : first + SMALL], aa, slots(idx, first, first + SMALL))
+            nc.sync.dma_start(out[:, first : first + SMALL], y[:, first : first + SMALL])
         nc.scalar.dma_start(out[:, HALF:], y[:, HALF:])

@@ -158,10 +158,12 @@ def tile_attend_tworelays_two_kernel(
             )
             b_banks.append(bank)
 
-        a_picked = sb.tile([P, I], F32, name="a_picked")
-        nc.vector.tensor_copy(a_picked[:, :HALF], a[:].indirect(slots(idx, 0, HALF)))
-        gather_scalar(a_picked[:, HALF:], a, slots(idx, HALF, I))
-        scatter(f1, idx2[:], a_picked[:])
+        to_f1_a = sb.tile([P, SMALL], F32, name="to_f1_a")
+        to_f1_b = sb.tile([P, I - SMALL], F32, name="to_f1_b")
+        gather_small(to_f1_a[:], a, slots(idx, 0, SMALL))
+        gather_scalar(to_f1_b[:], a, slots(idx, SMALL, I))
+        scatter(f1, slots(idx2, 0, SMALL), to_f1_a[:])
+        scatter(f1, slots(idx2, SMALL, I), to_f1_b[:])
 
         b_tail = sb.tile([P, U - SPLIT], F32, name="b_tail")
         nc.scalar.activation(b_tail[:], b_banks[1][:, SPLIT - NOTE_CHUNK :], COPY)

from contextlib import ExitStack

import concourse.mybir as mybir

D, T, U, I, Q = 512, 1024, 1024, 512, 128
FLOPS = 2 * D * Q * (T + U)

F32 = mybir.dt.float32
BF16 = mybir.dt.bfloat16
I32 = mybir.dt.int32
U32 = mybir.dt.uint32
U16 = mybir.dt.uint16
U8 = mybir.dt.uint8
FP8X4 = mybir.dt.float8_e4m3fn_x4
FP4X4 = mybir.dt.float4_e2m1fn_x4
ALU = mybir.AluOpType
COPY = mybir.ActivationFunctionType.Copy

P = 128
PACK = 4
QUADS = 4
QUAD_ROWS = 4
LIST_ROWS = 16
HALF = I // 2
SMALL = 128
KEY_CHUNK = 256
NOTE_CHUNK = 512
SPLIT = 704
KEY_LOADS = ((0, 256), (256, 256), (512, 512))
KEY_MATMULS = ((0, 256), (256, 256), (512, 256), (768, 128), (896, 128))


def slots(lst, lo, hi):
    return lst[:, lo // LIST_ROWS : hi // LIST_ROWS]


def tile_attend_tworelays_two_kernel(
    tc, query, keys_words, keys_scales, notes_words, notes_scales, offs, offs2, offs3, offs4, offs5, offs6, out
):
    nc = tc.nc
    with ExitStack() as ctx:
        lists = ctx.enter_context(tc.tile_pool(name="lists", bufs=1))
        sb = ctx.enter_context(tc.tile_pool(name="sb", bufs=1))
        psum = ctx.enter_context(tc.psum_pool(name="psum", bufs=1))

        def load_list(src, name):
            lst = lists.tile([P, I // LIST_ROWS], U16, name=name)
            nc.sync.dma_start(lst[:], src)
            return lst

        def gather_small(dst, window, offsets):
            nc.vector.tensor_tensor(dst, window[:].indirect(offsets), ones[:], ALU.mult)

        def gather_scalar(dst, window, offsets):
            nc.scalar.activation(dst, window[:].indirect(offsets), COPY)

        def scatter(window, offsets, src):
            nc.vector.tensor_copy(window[:].indirect(offsets), src)

        q_raw = sb.tile([P, PACK, Q], F32, name="q_raw")
        nc.sync.dma_start(q_raw[:], query.rearrange("(p j) q -> p j q", j=PACK))

        key_scales = sb.tile([P, KEY_CHUNK], U8, name="key_scales", align_bytes=64)
        ks_rows = keys_scales[0].bitcast(I32)
        planes = T // KEY_CHUNK
        for quad in range(QUADS):
            queue = nc.sync if quad < QUADS // 2 else nc.scalar
            queue.dma_start(
                key_scales[32 * quad : 32 * quad + planes * QUAD_ROWS, :].bitcast(I32),
                ks_rows[QUAD_ROWS * quad : QUAD_ROWS * (quad + 1), :].rearrange("r (c n) -> c r n", c=planes),
            )

        kw_rows = keys_words[0].rearrange("p n t -> p (n t)").bitcast(I32)
        key_words = []
        for first, width in KEY_LOADS:
            words = sb.tile([P, width], U32, name="key_words%d" % first, align_bytes=64)
            nc.sync.dma_start(words[:].bitcast(I32), kw_rows[:, first : first + width])
            key_words.append(words)

        idx = load_list(offs, "idx")
        idx2 = load_list(offs2, "idx2")

        f1 = sb.tile([P, U], F32, name="f1")
        nc.gpsimd.memset(f1[:], 0.0)
        f2 = sb.tile([P, T], F32, name="f2")
        nc.vector.memset(f2[:], 0.0)
        ones = sb.tile([P, SMALL], F32, name="ones")
        nc.vector.memset(ones[:], 1.0)

        note_words = sb.tile([P, 2 * U], U8, name="note_words", align_bytes=64)
        nc.sync.dma_start(note_words[:].bitcast(I32), notes_words[0].bitcast(I32))
        note_scales = sb.tile([P, U], U8, name="note_scales", align_bytes=64)
        ns_rows = notes_scales[0].bitcast(I32)
        for quad in range(QUADS):
            nc.sync.dma_start(
                note_scales[32 * quad : 32 * quad + QUAD_ROWS, :].bitcast(I32),
                ns_rows[QUAD_ROWS * quad : QUAD_ROWS * (quad + 1), :],
            )
        idx3 = load_list(offs3, "idx3")
        idx5 = load_list(offs5, "idx5")
        idx4 = load_list(offs4, "idx4")
        idx6 = load_list(offs6, "idx6")

        q_bf = sb.tile([P, Q, PACK], BF16, name="q_bf", tag="q_bf_then_f3", align_bytes=64)
        q_words = sb.tile([P, Q], U32, name="q_words", align_bytes=64)
        q_scales = sb.tile([P, Q], U8, name="q_scales", align_bytes=64)
        q_halves = (slice(0, Q // 2), slice(Q // 2, Q))
        for rows in q_halves:
            nc.vector.tensor_copy(
                q_bf[:, rows, :].rearrange("p (c i) j -> p c j i", i=4),
                q_raw[:, :, rows].rearrange("p j (c i) -> p c j i", i=4),
            )
        for rows in q_halves:
            nc.vector.quantize_mx(
                out=q_words[:, rows].bitcast(FP8X4),
                scales=q_scales[:, rows],
                in_=q_bf[:, rows, :].rearrange("p q j -> p (q j)"),
            )
        f3 = sb.tile([P, T], F32, name="f3", tag="q_bf_then_f3", align_bytes=64)
        nc.gpsimd.memset(f3[:], 0.0)

        def scores(bank, words, scales):
            nc.tensor.matmul_mx(
                out=bank[:],
                lhsT=q_words[:].bitcast(FP8X4),
                lhsT_scale=q_scales[:],
                rhs=words,
                rhs_scale=scales,
                start=True,
                stop=True,
            )

        a = sb.tile([P, T], F32, name="a")
        a_banks = []
        for n, (first, width) in enumerate(KEY_MATMULS):
            load = max(k for k, (lo, w) in enumerate(KEY_LOADS) if lo <= first)
            in_load = first - KEY_LOADS[load][0]
            plane, in_plane = divmod(first, KEY_CHUNK)
            bank = psum.tile([P, width], F32, name="a_bank%d" % first)
            scores(
                bank,
                key_words[load][:, in_load : in_load + width].bitcast(FP8X4),
                key_scales[QUAD_ROWS * plane : P, in_plane : in_plane + width],
            )
            a_banks.append(bank)
            if n % 2 == 0:
                nc.vector.tensor_copy(a[:, first : first + width], bank[:])
            else:
                nc.scalar.activation(a[:, first : first + width], bank[:], COPY)

        b_banks = []
        for first in range(0, U, NOTE_CHUNK):
            bank = psum.tile([P, NOTE_CHUNK], F32, name="b_bank%d" % first)
            scores(
                bank,
                note_words[:, 2 * first : 2 * (first + NOTE_CHUNK)].bitcast(FP4X4),
                note_scales[:, first : first + NOTE_CHUNK],
            )
            b_banks.append(bank)

        to_f1_a = sb.tile([P, SMALL], F32, name="to_f1_a")
        to_f1_b = sb.tile([P, I - SMALL], F32, name="to_f1_b")
        gather_small(to_f1_a[:], a, slots(idx, 0, SMALL))
        gather_scalar(to_f1_b[:], a, slots(idx, SMALL, I))
        scatter(f1, slots(idx2, 0, SMALL), to_f1_a[:])
        scatter(f1, slots(idx2, SMALL, I), to_f1_b[:])

        b_tail = sb.tile([P, U - SPLIT], F32, name="b_tail")
        nc.scalar.activation(b_tail[:], b_banks[1][:, SPLIT - NOTE_CHUNK :], COPY)
        bb = sb.tile([P, U], F32, name="bb")
        nc.gpsimd.tensor_tensor(bb[:, SPLIT:], b_tail[:], f1[:, SPLIT:], ALU.add)
        nc.vector.tensor_tensor(bb[:, :NOTE_CHUNK], b_banks[0][:], f1[:, :NOTE_CHUNK], ALU.add)
        nc.vector.tensor_tensor(
            bb[:, NOTE_CHUNK:SPLIT], b_banks[1][:, : SPLIT - NOTE_CHUNK], f1[:, NOTE_CHUNK:SPLIT], ALU.add
        )

        to_f2_a = sb.tile([P, SMALL], F32, name="to_f2_a")
        to_f2_b = sb.tile([P, I - SMALL], F32, name="to_f2_b")
        to_f3_a = sb.tile([P, HALF], F32, name="to_f3_a")
        to_f3_b = sb.tile([P, HALF], F32, name="to_f3_b")
        gather_small(to_f2_a[:], bb, slots(idx3, 0, SMALL))
        gather_scalar(to_f3_a[:], bb, slots(idx5, 0, HALF))
        gather_scalar(to_f2_b[:], bb, slots(idx3, SMALL, I))
        gather_scalar(to_f3_b[:], bb, slots(idx5, HALF, I))
        scatter(f2, slots(idx4, 0, SMALL), to_f2_a[:])
        scatter(f3, slots(idx6, 0, HALF), to_f3_a[:])
        scatter(f2, slots(idx4, SMALL, I), to_f2_b[:])
        scatter(f3, slots(idx6, HALF, I), to_f3_b[:])

        m1 = sb.tile([P, T], F32, name="m1")
        aa = sb.tile([P, T], F32, name="aa")
        for cols in (slice(0, KEY_CHUNK), slice(SPLIT, T), slice(KEY_CHUNK, SPLIT)):
            nc.vector.tensor_tensor(m1[:, cols], f2[:, cols], f3[:, cols], ALU.max)
        nc.gpsimd.tensor_tensor(aa[:, SPLIT:], a[:, SPLIT:], m1[:, SPLIT:], ALU.subtract)
        for bank, (first, width) in zip(a_banks, KEY_MATMULS):
            last = min(first + width, SPLIT)
            if first < last:
                nc.vector.tensor_tensor(aa[:, first:last], bank[:, : last - first], m1[:, first:last], ALU.subtract)

        y = sb.tile([P, I], F32, name="y")
        gather_scalar(y[:, HALF:], aa, slots(idx, HALF, I))
        for first in range(0, HALF, SMALL):
            gather_small(y[:, first : first + SMALL], aa, slots(idx, first, first + SMALL))
            nc.sync.dma_start(out[:, first : first + SMALL], y[:, first : first + SMALL])
        nc.scalar.dma_start(out[:, HALF:], y[:, HALF:])
